import numpy as np
import ml_dtypes


def mxq(x, axis, fmt="e4m3"):
    dtype, down = {"e4m3": (ml_dtypes.float8_e4m3fn, 7), "e5m2": (ml_dtypes.float8_e5m2, 14)}[fmt]
    v = np.moveaxis(np.asarray(x, np.float32).astype(ml_dtypes.bfloat16).astype(np.float64), axis, -1)
    blocks = v.reshape(v.shape[:-1] + (-1, 32))
    amax = np.abs(blocks).max(-1, keepdims=True)
    byte = np.maximum(np.where(amax > 0, np.frexp(amax)[1] - 1 + 127, 0) - down, 1)
    scale = np.exp2(byte - 127.0)
    codes = (blocks / scale).astype(np.float32).astype(dtype).astype(np.float64)
    return np.moveaxis((codes * scale).reshape(v.shape), -1, axis)


WIDE = False


def mx_kscale(k):
    if not WIDE:
        return np.ones(k)
    levels = np.array([10, -10, 5, -5, 0])
    if k % 512:
        return np.exp2(np.random.permutation(np.resize(levels, k // 32))).repeat(32)
    a = np.empty((k // 512, 16))
    for p in range(k // 512):
        a[p, :8] = np.random.permutation(np.resize(levels, 8))
        for g in range(8):
            far = levels[np.abs(levels - a[p, g]) >= 10]
            a[p, g + 8] = far[np.random.randint(len(far))]
    return np.exp2(a.ravel()).repeat(32)


def f64(x):
    return np.asarray(x).astype(np.float64)


def striped(idx):
    return np.tile(np.asarray(idx).reshape(-1, 16).T, (8, 1)).astype(np.uint16)


def unstriped(offs):
    return offs[:16].T.reshape(-1).astype(np.int64)


E2M1 = np.array([0.0, 0.5, 1.0, 1.5, 2.0, 3.0, 4.0, 6.0, -0.0, -0.5, -1.0, -1.5, -2.0, -3.0, -4.0, -6.0])


def pack_weight(w, fmt):
    k, n = w.shape
    w = f64(np.asarray(w, np.float32).astype(ml_dtypes.bfloat16)).reshape(k // 32, 32, n)
    amax = np.abs(w).max(1)
    if fmt == "e4m3":
        byte = np.frexp(amax)[1] - 1 + 127 - 7
    else:
        mant, ex = np.frexp(amax / 6.0)
        byte = np.where(mant > 0.5, ex, ex - 1) + 127
    byte = np.clip(np.where(amax > 0, byte, 1), 1, 254)
    scaled = (w * np.exp2(127.0 - byte)[:, None, :]).reshape(k, n).astype(np.float32)
    by_word = np.ascontiguousarray(scaled.reshape(k // 512, 128, 4, n).transpose(0, 1, 3, 2))
    if fmt == "e4m3":
        words = by_word.astype(ml_dtypes.float8_e4m3fn).view(np.uint8)
    else:
        c = by_word.astype(ml_dtypes.float4_e2m1fn).view(np.uint8) & 0xF
        words = (c[..., 0::2] | (c[..., 1::2] << 4)).reshape(k // 512, 128, 2 * n)
    return np.ascontiguousarray(words), np.ascontiguousarray(byte.astype(np.uint8).reshape(k // 512, 16, n))


def unpack_weight(words, scales, fmt):
    g, _, n = scales.shape
    words = np.ascontiguousarray(words).reshape(g, 128, n, -1)
    if fmt == "e4m3":
        vals = words.view(ml_dtypes.float8_e4m3fn).astype(np.float64)
    else:
        nib = np.empty((g, 128, n, 4), np.uint8)
        nib[..., 0::2] = words & 0xF
        nib[..., 1::2] = words >> 4
        vals = E2M1[nib]
    vals = vals * np.repeat(np.exp2(scales.astype(np.float64) - 127.0), 8, axis=1)[..., None]
    return vals.transpose(0, 1, 3, 2).reshape(g * 512, n)


def softplus(v):
    return np.log(1.0 + np.exp(v))


def sigmoid(v):
    return 1.0 / (1.0 + np.exp(-v))


K, R, F, T, J, M = 512, 128, 512, 2048, 512, 256


def setup_inputs():
    n = np.random.standard_normal
    idx = np.random.permutation(T)[:J]
    idx2 = np.random.permutation(J)[:M]
    idx3 = np.random.permutation(J)[:M]
    idx4 = np.random.permutation(J)[:M]
    fk = mx_kscale(K)
    ff = mx_kscale(F)
    tabp = pack_weight(n((K, T)) / fk[:, None], "e2m1")
    return {
        "tab_words": tabp[0],
        "tab_scales": tabp[1],
        "w1": (n((K, R)) * 1 / np.sqrt(K) * fk[:, None]).astype(np.float32),
        "bias": (np.random.uniform(-0.5, 0.5, (R, 1))).astype(np.float32),
        "wo": (n((F, R)) * 1 / np.sqrt(F) * ff[:, None]).astype(np.float32),
        "dy": (n((F, M)) / ff[:, None]).astype(np.float32),
        "og": (np.random.uniform(0.3, 1.0, (R, 1))).astype(np.float32),
        "base": (0.3 * n((R, J))).astype(np.float32),
        "offs": striped(idx),
        "offs2": striped(idx2),
        "offs3": striped(idx3),
        "offs4": striped(idx4),
    }


def reference(tab_words, tab_scales, w1, bias, wo, dy, og, base, offs, offs2, offs3, offs4):
    idx = unstriped(offs)
    idx2 = unstriped(offs2)
    idx3 = unstriped(offs3)
    idx4 = unstriped(offs4)
    tabu = unpack_weight(tab_words, tab_scales, "e2m1")
    w1q = mxq(f64(w1), 0, "e4m3")
    tabidxg = tabu[:, idx]
    a = w1q.T @ tabidxg
    h1 = softplus(a + f64(bias))
    s = h1[:, idx2] * h1[:, idx3] * h1[:, idx4]
    woq = mxq(f64(wo), 0, "e4m3")
    dyq = mxq(f64(dy), 0, "e4m3")
    c0 = woq.T @ dyq
    ds = c0 / (s + 1.0)
    e1 = ds * h1[:, idx4] * h1[:, idx3]
    s1 = np.zeros((R, J))
    s1[:, idx2] = e1
    e2 = ds * h1[:, idx4] * h1[:, idx2]
    s2 = np.zeros((R, J))
    s2[:, idx3] = e2
    e3 = ds * h1[:, idx2] * h1[:, idx3]
    s3 = np.zeros((R, J))
    s3[:, idx4] = e3
    dh1 = s1 + s2 + s3
    da = dh1 * sigmoid(a + f64(bias))
    hda = da * 2.0
    hdh1 = hda * sigmoid(a + f64(bias))
    he3 = hdh1[:, idx4]
    he2 = hdh1[:, idx3]
    he1 = hdh1[:, idx2]
    hds = he3 * h1[:, idx2] * h1[:, idx3] + he2 * h1[:, idx2] * h1[:, idx4] + he1 * h1[:, idx3] * h1[:, idx4]
    hs = hds * c0 / np.square(s + 1.0) * (-1.0)
    e51 = he3 * ds * h1[:, idx3]
    s51 = np.zeros((R, J))
    s51[:, idx2] = e51
    e52 = he2 * ds * h1[:, idx4]
    s52 = np.zeros((R, J))
    s52[:, idx2] = e52
    e53 = hs * h1[:, idx4] * h1[:, idx3]
    s53 = np.zeros((R, J))
    s53[:, idx2] = e53
    e54 = he3 * ds * h1[:, idx2]
    s54 = np.zeros((R, J))
    s54[:, idx3] = e54
    e55 = he1 * ds * h1[:, idx4]
    s55 = np.zeros((R, J))
    s55[:, idx3] = e55
    e56 = hs * h1[:, idx4] * h1[:, idx2]
    s56 = np.zeros((R, J))
    s56[:, idx3] = e56
    e57 = he2 * h1[:, idx2] * ds
    s57 = np.zeros((R, J))
    s57[:, idx4] = e57
    e58 = he1 * h1[:, idx3] * ds
    s58 = np.zeros((R, J))
    s58[:, idx4] = e58
    e59 = hs * h1[:, idx2] * h1[:, idx3]
    s59 = np.zeros((R, J))
    s59[:, idx4] = e59
    hh1 = s51 + s52 + s53 + s54 + s55 + s56 + s57 + s58 + s59
    ha = hda * dh1 * sigmoid(a + f64(bias)) * (1.0 - sigmoid(a + f64(bias))) + hh1 * sigmoid(a + f64(bias))
    y = ha * f64(og) + f64(base)
    return y

@@ -1,0 +1,202 @@
+import math
+from contextlib import ExitStack
+
+import concourse.mybir as mybir
+
+K, R, F, T, J, M = 512, 128, 512, 2048, 512, 256
+FLOPS = 2 * K * R * J + 2 * F * R * M
+
+F32 = mybir.dt.float32
+BF16 = mybir.dt.bfloat16
+I32 = mybir.dt.int32
+U32 = mybir.dt.uint32
+U16 = mybir.dt.uint16
+U8 = mybir.dt.uint8
+FP8X4 = mybir.dt.float8_e4m3fn_x4
+FP4X4 = mybir.dt.float4_e2m1fn_x4
+ALU = mybir.AluOpType
+ACT = mybir.ActivationFunctionType
+
+P = 128
+PACK = 4
+HALF = J // 2
+TINY = 2.0 ** -63
+
+
+def tile_attend_gptriples_kernel(tc, tab_words, tab_scales, w1, bias, wo, dy, og, base, offs, offs2, offs3, offs4, out):
+    nc = tc.nc
+    mult, add, sub, amax = ALU.mult, ALU.add, ALU.subtract, ALU.max
+    halves = [slice(0, HALF), slice(HALF, J)]
+
+    with ExitStack() as ctx:
+        lists = ctx.enter_context(tc.tile_pool(name="lists", bufs=1))
+        sb = ctx.enter_context(tc.tile_pool(name="sb", bufs=1))
+        ps = ctx.enter_context(tc.psum_pool(name="ps", bufs=1))
+
+        def interleave(engine_copy, dst, src):
+            engine_copy(out=dst.rearrange("p (c i) t -> p c t i", i=4), in_=src.rearrange("p t (c i) -> p c t i", i=4))
+
+        scales = sb.tile([P, T], U8, align_bytes=64)
+        l1 = lists.tile([P, J // 16], U16)
+        nc.sync.dma_start(l1[:], offs)
+        for quad in range(4):
+            rows = tab_scales[0, 4 * quad : 4 * quad + 4, :].bitcast(I32)
+            nc.sync.dma_start(out=scales[32 * quad : 32 * quad + 32, :].bitcast(I32), in_=rows.partition_broadcast(8))
+        w1_raw = sb.tile([P, PACK, R], F32)
+        nc.sync.dma_start(out=w1_raw[:], in_=w1.rearrange("(p t) r -> p t r", t=PACK))
+        words = sb.tile([P, T], U16, align_bytes=64)
+        nc.sync.dma_start(out=words[:].bitcast(I32), in_=tab_words[0].bitcast(I32))
+        bias_t = sb.tile([P, 1], F32)
+        nc.sync.dma_start(out=bias_t[:], in_=bias)
+        wo_raw = sb.tile([P, PACK, R], F32)
+        nc.sync.dma_start(out=wo_raw[:], in_=wo.rearrange("(p t) r -> p t r", t=PACK))
+        dy_raw = sb.tile([P, PACK, M], F32)
+        nc.sync.dma_start(out=dy_raw[:], in_=dy.rearrange("(p t) m -> p t m", t=PACK))
+        l2 = lists.tile([P, M // 16], U16)
+        nc.sync.dma_start(l2[:], offs2)
+        l3 = lists.tile([P, M // 16], U16)
+        nc.sync.dma_start(l3[:], offs3)
+        l4 = lists.tile([P, M // 16], U16)
+        nc.sync.dma_start(l4[:], offs4)
+        og_t = sb.tile([P, 1], F32)
+        nc.sync.dma_start(out=og_t[:], in_=og)
+        base_t = sb.tile([P, J], F32)
+        nc.sync.dma_start(out=base_t[:], in_=base)
+
+        win2 = sb.tile([P, J], F32)
+        win3 = sb.tile([P, J], F32)
+        win4 = sb.tile([P, J], F32)
+        for win in (win2, win3, win4):
+            nc.gpsimd.memset(win[:], 0.0)
+
+        g_scales = sb.tile([P, J], U8, align_bytes=64)
+        nc.vector.tensor_copy(g_scales[:], scales[:].indirect(l1[:]))
+        w1_bf = sb.tile([P, R, PACK], BF16, align_bytes=64)
+        interleave(nc.scalar.copy, w1_bf[:], w1_raw[:])
+        w1_codes = sb.tile([P, R], U32, align_bytes=64)
+        w1_scales = sb.tile([P, R], U8, align_bytes=64)
+        nc.vector.quantize_mx(out=w1_codes[:].bitcast(FP8X4), scales=w1_scales[:], in_=w1_bf[:].rearrange("p r t -> p (r t)"))
+        neg_bias = sb.tile([P, 1], F32, tag="neg_bias")
+        nc.gpsimd.tensor_scalar(neg_bias[:], bias_t[:], -1.0, 0.0, mult, add)
+
+        g_words = sb.tile([P, J], U16, align_bytes=64)
+        sig_neg = sb.tile([P, J], F32)
+        a_ps = []
+        for n, cols in enumerate(halves):
+            nc.vector.tensor_copy(g_words[:, cols], words[:].indirect(l1[:, n * (HALF // 16) : (n + 1) * (HALF // 16)]))
+            bank = ps.tile([P, HALF], F32, name="a_bank%d" % n)
+            nc.tensor.matmul_mx(out=bank[:], lhsT=w1_codes[:].bitcast(FP8X4), lhsT_scale=w1_scales[:],
+                                rhs=g_words[:, cols].bitcast(FP4X4), rhs_scale=g_scales[:, cols], start=True, stop=True)
+            nc.scalar.activation(sig_neg[:, cols], bank[:], ACT.Sigmoid, bias=neg_bias[:], scale=-1.0)
+            a_ps.append(bank)
+
+        log_neg = [sb.tile([P, HALF], F32, tag="neg_bias", name="log0"), sb.tile([P, HALF], F32, name="log1")]
+        pre = sb.tile([P, J], F32)
+        h1 = sb.tile([P, J], F32)
+        for n, cols in enumerate(halves):
+            nc.scalar.activation(log_neg[n][:], sig_neg[:, cols], ACT.Ln, bias=TINY)
+            nc.vector.tensor_scalar(pre[:, cols], a_ps[n][:], bias_t[:], None, add)
+        for n, cols in enumerate(halves):
+            nc.vector.scalar_tensor_tensor(h1[:, cols], log_neg[n][:], -1.0, pre[:, cols], mult, amax)
+
+        last_bf = sb.tile([P, R + M, PACK], BF16, align_bytes=64)
+        interleave(nc.vector.tensor_copy, last_bf[:, 0:R, :], wo_raw[:])
+        interleave(nc.vector.tensor_copy, last_bf[:, R : R + M, :], dy_raw[:])
+        last_codes = sb.tile([P, R + M], U32, align_bytes=64)
+        last_scales = sb.tile([P, R + M], U8, align_bytes=64)
+        nc.vector.quantize_mx(out=last_codes[:].bitcast(FP8X4), scales=last_scales[:], in_=last_bf[:].rearrange("p c t -> p (c t)"))
+        c0 = ps.tile([P, M], F32)
+        nc.tensor.matmul_mx(out=c0[:], lhsT=last_codes[:, 0:R].bitcast(FP8X4), lhsT_scale=last_scales[:, 0:R],
+                            rhs=last_codes[:, R : R + M].bitcast(FP8X4), rhs_scale=last_scales[:, R : R + M], start=True, stop=True)
+        sig = sb.tile([P, J], F32)
+        nc.vector.tensor_scalar(sig[:], sig_neg[:], -1.0, 1.0, mult, add)
+        sig_sq = sb.tile([P, J], F32)
+        nc.vector.tensor_tensor(sig_sq[:], sig[:], sig[:], mult)
+
+        hg = sb.tile([P, 3, M], F32)
+        hc, hb, ha = hg[:, 0, :], hg[:, 1, :], hg[:, 2, :]
+        nc.scalar.activation(hc, h1[:].indirect(l4[:]), ACT.Copy)
+        nc.vector.tensor_copy(ha, h1[:].indirect(l2[:]))
+        nc.vector.tensor_copy(hb, h1[:].indirect(l3[:]))
+        pair = sb.tile([P, 3, M], F32)
+        nc.vector.tensor_tensor(pair[:, 2, :], ha, hb, mult)
+        s = sb.tile([P, M], F32)
+        nc.vector.tensor_tensor(s[:], pair[:, 2, :], hc, mult)
+        root = sb.tile([P, M], F32, tag="root")
+        nc.scalar.activation(root[:], s[:], ACT.Abs_reciprocal_sqrt, bias=1.0)
+        rec = sb.tile([P, M], F32)
+        nc.scalar.activation(rec[:], root[:], ACT.Square)
+        c_ab = sb.tile([P, M], F32)
+        nc.vector.tensor_tensor(c_ab[:], c0[:], pair[:, 2, :], mult)
+        nc.vector.tensor_tensor(pair[:, 1, :], ha, hc, mult)
+        nc.vector.tensor_tensor(pair[:, 0, :], hb, hc, mult)
+
+        e3 = sb.tile([P, M], F32)
+        nc.vector.tensor_tensor(e3[:], c_ab[:], rec[:], mult)
+        nc.scalar.activation(win4[:].indirect(l4[:]), e3[:], ACT.Copy)
+        ds = sb.tile([P, M], F32)
+        nc.vector.tensor_tensor(ds[:], c0[:], rec[:], mult)
+        e2 = sb.tile([P, M], F32, tag="e2")
+        nc.vector.tensor_tensor(e2[:], ds[:], pair[:, 1, :], mult)
+        nc.scalar.activation(win3[:].indirect(l3[:]), e2[:], ACT.Copy)
+        nc.vector.tensor_tensor(win2[:].indirect(l2[:]), ds[:], pair[:, 0, :], mult)
+        gain = sb.tile([P, M], F32, tag="gain")
+        nc.vector.tensor_tensor(gain[:], ds[:], rec[:], mult)
+        ab_sq = sb.tile([P, M], F32, tag="root")
+        nc.scalar.activation(ab_sq[:], pair[:, 2, :], ACT.Square)
+        rest_sq = sb.tile([P, 2, M], F32, tag="e2")
+        nc.scalar.activation(rest_sq[:], pair[:, 0:2, :], ACT.Square)
+        dh1 = sb.tile([P, J], F32)
+        nc.vector.tensor_tensor(dh1[:], win2[:], win4[:], add)
+        for cols in halves:
+            nc.vector.tensor_tensor(dh1[:, cols], dh1[:, cols], win3[:, cols], add)
+        hdh1 = sb.tile([P, J], F32, tag="hdh1")
+        for cols in halves:
+            nc.vector.scalar_tensor_tensor(hdh1[:, cols], dh1[:, cols], 2.0, sig_sq[:, cols], mult, mult)
+        dh1_sq = sb.tile([P, J], F32)
+        nc.scalar.activation(dh1_sq[:], dh1[:], ACT.Square, scale=math.sqrt(0.5))
+
+        he = sb.tile([P, 3, M], F32)
+        he1, he2, he3 = he[:, 0, :], he[:, 1, :], he[:, 2, :]
+        nc.scalar.activation(he2, hdh1[:].indirect(l3[:]), ACT.Copy)
+        nc.vector.tensor_copy(he1[:, 0 : M // 2], hdh1[:].indirect(l2[:, 0 : M // 32]))
+        nc.scalar.activation(he1[:, M // 2 : M], hdh1[:].indirect(l2[:, M // 32 : M // 16]), ACT.Copy)
+        nc.scalar.activation(he3, hdh1[:].indirect(l4[:]), ACT.Copy)
+        centred_sq = sb.tile([P, J], F32, tag="hdh1")
+        nc.scalar.activation(centred_sq[:], sig_neg[:], ACT.Square, bias=1.0, scale=-2.0)
+
+        x4 = sb.tile([P, 3, M], F32)
+        x2 = sb.tile([P, 3, M], F32)
+        x3 = sb.tile([P, 3, M], F32)
+
+        def finish(x, win, lst):
+            nc.vector.tensor_tensor(x[:, 0, :], x[:, 0, :], x[:, 1, :], add)
+            nc.vector.tensor_tensor(x[:, 0, :], x[:, 0, :], x[:, 2, :], sub)
+            nc.vector.tensor_tensor(x[:, 0, :], x[:, 0, :], gain[:], mult)
+            nc.scalar.activation(win[:].indirect(lst[:]), x[:, 0, :], ACT.Copy)
+
+        nc.vector.tensor_tensor(x4[:, 1, :], ha, he2, mult)
+        nc.vector.tensor_tensor(x4[:, 0, :], hb, he1, mult)
+        nc.vector.tensor_tensor(x4[:, 2, :], ab_sq[:], he3, mult)
+        finish(x4, win4, l4)
+        nc.vector.tensor_tensor(x2[:, 2, :], rest_sq[:, 0, :], he1, mult)
+        nc.vector.tensor_tensor(x2[:, 0, :], hc, he2, mult)
+        nc.vector.tensor_tensor(x2[:, 1, :], hb, he3, mult)
+        finish(x2, win2, l2)
+        nc.vector.tensor_tensor(x3[:, 2, :], rest_sq[:, 1, :], he2, mult)
+        nc.vector.tensor_tensor(x3[:, 0, :], hc, he1, mult)
+        nc.vector.tensor_tensor(x3[:, 1, :], ha, he3, mult)
+        finish(x3, win3, l3)
+
+        total = sb.tile([P, J], F32, tag="gain")
+        nc.vector.scalar_tensor_tensor(total[:], centred_sq[:], 1.0, dh1_sq[:], sub, mult)
+        for cols in halves:
+            nc.vector.tensor_tensor(total[:, cols], win4[:, cols], total[:, cols], sub)
+        for win in (win2, win3):
+            for cols in halves:
+                nc.vector.tensor_tensor(total[:, cols], total[:, cols], win[:, cols], add)
+        for cols in halves:
+            nc.vector.scalar_tensor_tensor(total[:, cols], total[:, cols], og_t[:], sig[:, cols], mult, mult)
+        for cols in halves:
+            nc.vector.tensor_tensor(total[:, cols], total[:, cols], base_t[:, cols], add)
+            nc.sync.dma_start(out=out[:, cols], in_=total[:, cols])

@@ -69,6 +69,10 @@ def tile_attend_gptriples_kernel(tc, tab_words, tab_scales, w1, bias, wo, dy, og
         for win in (win2, win3, win4):
             nc.gpsimd.memset(win[:], 0.0)
 
+        warm_in = sb.tile([P, 1], F32)
+        nc.gpsimd.memset(warm_in[:], 1.0)
+        warm_sig = sb.tile([P, 1], F32)
+        nc.scalar.activation(warm_sig[:], warm_in[:], ACT.Sigmoid)
         g_scales = sb.tile([P, J], U8, align_bytes=64)
         nc.vector.tensor_copy(g_scales[:], scales[:].indirect(l1[:]))
         w1_bf = sb.tile([P, R, PACK], BF16, align_bytes=64)
@@ -116,6 +120,8 @@ def tile_attend_gptriples_kernel(tc, tab_words, tab_scales, w1, bias, wo, dy, og
         hg = sb.tile([P, 3, M], F32)
         hc, hb, ha = hg[:, 0, :], hg[:, 1, :], hg[:, 2, :]
         nc.scalar.activation(hc, h1[:].indirect(l4[:]), ACT.Copy)
+        warm_root = sb.tile([P, 1], F32)
+        nc.scalar.activation(warm_root[:], hg[:, 0, 0:1], ACT.Abs_reciprocal_sqrt, bias=1.0)
         nc.vector.tensor_copy(ha, h1[:].indirect(l2[:]))
         nc.vector.tensor_copy(hb, h1[:].indirect(l3[:]))
         pair = sb.tile([P, 3, M], F32)

@@ -20,6 +20,7 @@ ACT = mybir.ActivationFunctionType
 P = 128
 PACK = 4
 HALF = J // 2
+SHARE = 64
 TINY = 2.0 ** -63
 
 
@@ -50,7 +51,7 @@ def tile_attend_gptriples_kernel(tc, tab_words, tab_scales, w1, bias, wo, dy, og
         nc.sync.dma_start(out=bias_t[:], in_=bias)
         wo_raw = sb.tile([P, PACK, R], F32)
         nc.sync.dma_start(out=wo_raw[:], in_=wo.rearrange("(p t) r -> p t r", t=PACK))
-        dy_raw = sb.tile([P, PACK, M], F32)
+        dy_raw = sb.tile([P, PACK, M], F32, tag="dy_raw")
         nc.sync.dma_start(out=dy_raw[:], in_=dy.rearrange("(p t) m -> p t m", t=PACK))
         l2 = lists.tile([P, M // 16], U16)
         nc.sync.dma_start(l2[:], offs2)
@@ -78,10 +79,10 @@ def tile_attend_gptriples_kernel(tc, tab_words, tab_scales, w1, bias, wo, dy, og
         w1_bf = sb.tile([P, R, PACK], BF16, align_bytes=64)
         interleave(nc.scalar.copy, w1_bf[:], w1_raw[:])
         w1_codes = sb.tile([P, R], U32, align_bytes=64)
-        w1_scales = sb.tile([P, R], U8, align_bytes=64)
+        w1_scales = sb.tile([P, R], U8, align_bytes=64, tag="w1_scales")
         nc.vector.quantize_mx(out=w1_codes[:].bitcast(FP8X4), scales=w1_scales[:], in_=w1_bf[:].rearrange("p r t -> p (r t)"))
-        neg_bias = sb.tile([P, 1], F32, tag="neg_bias")
-        nc.gpsimd.tensor_scalar(neg_bias[:], bias_t[:], -1.0, 0.0, mult, add)
+        neg_bias = sb.tile([P, 1], F32)
+        nc.scalar.activation(neg_bias[:], bias_t[:], ACT.Copy, scale=-1.0)
 
         g_words = sb.tile([P, J], U16, align_bytes=64)
         sig_neg = sb.tile([P, J], F32)
@@ -94,16 +95,7 @@ def tile_attend_gptriples_kernel(tc, tab_words, tab_scales, w1, bias, wo, dy, og
             nc.scalar.activation(sig_neg[:, cols], bank[:], ACT.Sigmoid, bias=neg_bias[:], scale=-1.0)
             a_ps.append(bank)
 
-        log_neg = [sb.tile([P, HALF], F32, tag="neg_bias", name="log0"), sb.tile([P, HALF], F32, name="log1")]
-        pre = sb.tile([P, J], F32)
-        h1 = sb.tile([P, J], F32)
-        for n, cols in enumerate(halves):
-            nc.scalar.activation(log_neg[n][:], sig_neg[:, cols], ACT.Ln, bias=TINY)
-            nc.vector.tensor_scalar(pre[:, cols], a_ps[n][:], bias_t[:], None, add)
-        for n, cols in enumerate(halves):
-            nc.vector.scalar_tensor_tensor(h1[:, cols], log_neg[n][:], -1.0, pre[:, cols], mult, amax)
-
-        last_bf = sb.tile([P, R + M, PACK], BF16, align_bytes=64)
+        last_bf = sb.tile([P, R + M, PACK], BF16, align_bytes=64, tag="last_bf")
         interleave(nc.vector.tensor_copy, last_bf[:, 0:R, :], wo_raw[:])
         interleave(nc.vector.tensor_copy, last_bf[:, R : R + M, :], dy_raw[:])
         last_codes = sb.tile([P, R + M], U32, align_bytes=64)
@@ -112,97 +104,109 @@ def tile_attend_gptriples_kernel(tc, tab_words, tab_scales, w1, bias, wo, dy, og
         c0 = ps.tile([P, M], F32)
         nc.tensor.matmul_mx(out=c0[:], lhsT=last_codes[:, 0:R].bitcast(FP8X4), lhsT_scale=last_scales[:, 0:R],
                             rhs=last_codes[:, R : R + M].bitcast(FP8X4), rhs_scale=last_scales[:, R : R + M], start=True, stop=True)
-        sig = sb.tile([P, J], F32)
+        log_neg = [sb.tile([P, HALF], F32, align_bytes=64, tag="w1_scales", name="log0"), sb.tile([P, HALF], F32, tag="log1", name="log1")]
+        pre = sb.tile([P, J], F32, tag="dy_raw")
+        h1 = sb.tile([P, J], F32)
+        for n, cols in enumerate(halves):
+            nc.scalar.activation(log_neg[n][:], sig_neg[:, cols], ACT.Ln, bias=TINY)
+            nc.vector.tensor_scalar(pre[:, cols], a_ps[n][:], bias_t[:], None, add)
+        for n, cols in enumerate(halves):
+            nc.vector.scalar_tensor_tensor(h1[:, cols], log_neg[n][:], -1.0, pre[:, cols], mult, amax)
+
+        sig = sb.tile([P, J], F32, align_bytes=64, tag="last_bf")
         nc.vector.tensor_scalar(sig[:], sig_neg[:], -1.0, 1.0, mult, add)
-        sig_sq = sb.tile([P, J], F32)
+        sig_sq = sb.tile([P, J], F32, tag="sig_sq")
         nc.vector.tensor_tensor(sig_sq[:], sig[:], sig[:], mult)
 
         hg = sb.tile([P, 3, M], F32)
         hc, hb, ha = hg[:, 0, :], hg[:, 1, :], hg[:, 2, :]
-        nc.scalar.activation(hc, h1[:].indirect(l4[:]), ACT.Copy)
-        warm_root = sb.tile([P, 1], F32)
-        nc.scalar.activation(warm_root[:], hg[:, 0, 0:1], ACT.Abs_reciprocal_sqrt, bias=1.0)
-        nc.vector.tensor_copy(ha, h1[:].indirect(l2[:]))
+        nc.scalar.activation(ha, h1[:].indirect(l2[:]), ACT.Copy)
+        warm_root = sb.tile([P, 1], F32, tag="log1")
+        nc.scalar.activation(warm_root[:], warm_in[:], ACT.Abs_reciprocal_sqrt, bias=1.0)
         nc.vector.tensor_copy(hb, h1[:].indirect(l3[:]))
-        pair = sb.tile([P, 3, M], F32)
-        nc.vector.tensor_tensor(pair[:, 2, :], ha, hb, mult)
-        s = sb.tile([P, M], F32)
-        nc.vector.tensor_tensor(s[:], pair[:, 2, :], hc, mult)
-        root = sb.tile([P, M], F32, tag="root")
+        nc.vector.tensor_copy(hc, h1[:].indirect(l4[:]))
+        ab = sb.tile([P, M], F32)
+        nc.vector.tensor_tensor(ab[:], ha, hb, mult)
+        s = sb.tile([P, M], F32, tag="s")
+        nc.vector.tensor_tensor(s[:], ab[:], hc, mult)
+        root = sb.tile([P, M], F32)
         nc.scalar.activation(root[:], s[:], ACT.Abs_reciprocal_sqrt, bias=1.0)
         rec = sb.tile([P, M], F32)
         nc.scalar.activation(rec[:], root[:], ACT.Square)
         c_ab = sb.tile([P, M], F32)
-        nc.vector.tensor_tensor(c_ab[:], c0[:], pair[:, 2, :], mult)
-        nc.vector.tensor_tensor(pair[:, 1, :], ha, hc, mult)
-        nc.vector.tensor_tensor(pair[:, 0, :], hb, hc, mult)
+        nc.vector.tensor_tensor(c_ab[:], c0[:], ab[:], mult)
+        c_c = sb.tile([P, M], F32)
+        nc.vector.tensor_tensor(c_c[:], c0[:], hc, mult)
+        c_pair = sb.tile([P, 2, M], F32, tag="c_pair")
+        c_bc, c_ac = c_pair[:, 0, :], c_pair[:, 1, :]
+        nc.vector.tensor_tensor(c_pair[:], hg[:, 1:3, :], c_c[:].unsqueeze(1).to_broadcast([P, 2, M]), mult)
 
+        e1 = sb.tile([P, M], F32)
+        e2 = sb.tile([P, M], F32)
         e3 = sb.tile([P, M], F32)
         nc.vector.tensor_tensor(e3[:], c_ab[:], rec[:], mult)
         nc.scalar.activation(win4[:].indirect(l4[:]), e3[:], ACT.Copy)
-        ds = sb.tile([P, M], F32)
-        nc.vector.tensor_tensor(ds[:], c0[:], rec[:], mult)
-        e2 = sb.tile([P, M], F32, tag="e2")
-        nc.vector.tensor_tensor(e2[:], ds[:], pair[:, 1, :], mult)
-        nc.scalar.activation(win3[:].indirect(l3[:]), e2[:], ACT.Copy)
-        nc.vector.tensor_tensor(win2[:].indirect(l2[:]), ds[:], pair[:, 0, :], mult)
-        gain = sb.tile([P, M], F32, tag="gain")
-        nc.vector.tensor_tensor(gain[:], ds[:], rec[:], mult)
-        ab_sq = sb.tile([P, M], F32, tag="root")
-        nc.scalar.activation(ab_sq[:], pair[:, 2, :], ACT.Square)
-        rest_sq = sb.tile([P, 2, M], F32, tag="e2")
-        nc.scalar.activation(rest_sq[:], pair[:, 0:2, :], ACT.Square)
+        nc.vector.tensor_tensor(win3[:].indirect(l3[:, 0 : SHARE // 16]), c_ac[:, 0:SHARE], rec[:, 0:SHARE], mult)
+        nc.vector.tensor_tensor(e2[:], c_ac, rec[:], mult)
+        nc.scalar.activation(win3[:].indirect(l3[:, SHARE // 16 : M // 16]), e2[:, SHARE:M], ACT.Copy)
+        nc.vector.tensor_tensor(win2[:].indirect(l2[:]), c_bc, rec[:], mult)
         dh1 = sb.tile([P, J], F32)
-        nc.vector.tensor_tensor(dh1[:], win2[:], win4[:], add)
+        for cols in halves:
+            nc.vector.tensor_tensor(dh1[:, cols], win2[:, cols], win4[:, cols], add)
+        nc.vector.tensor_tensor(e1[:], c_bc, rec[:], mult)
+        early = sb.tile([P, M + J], F32, tag="s")
+        c_sq, centred_sq = early[:, 0:M], early[:, M : M + J]
+        nc.scalar.activation(c_sq, hc, ACT.Square)
+        nc.scalar.activation(centred_sq, sig_neg[:], ACT.Square, bias=1.0, scale=-2.0)
+        ba_sq = sb.tile([P, 2, M], F32, tag="c_pair")
+        nc.scalar.activation(ba_sq[:], hg[:, 1:3, :], ACT.Square)
+        inv = sb.tile([P, 2, M], F32)
+        nc.scalar.activation(inv[:], ba_sq[:], ACT.Abs_reciprocal_sqrt, bias=TINY)
         for cols in halves:
             nc.vector.tensor_tensor(dh1[:, cols], dh1[:, cols], win3[:, cols], add)
         hdh1 = sb.tile([P, J], F32, tag="hdh1")
         for cols in halves:
             nc.vector.scalar_tensor_tensor(hdh1[:, cols], dh1[:, cols], 2.0, sig_sq[:, cols], mult, mult)
-        dh1_sq = sb.tile([P, J], F32)
-        nc.scalar.activation(dh1_sq[:], dh1[:], ACT.Square, scale=math.sqrt(0.5))
+        total = sb.tile([P, J], F32)
+        nc.scalar.activation(total[:], dh1[:], ACT.Square, scale=math.sqrt(0.5))
 
-        he = sb.tile([P, 3, M], F32)
-        he1, he2, he3 = he[:, 0, :], he[:, 1, :], he[:, 2, :]
-        nc.scalar.activation(he2, hdh1[:].indirect(l3[:]), ACT.Copy)
-        nc.vector.tensor_copy(he1[:, 0 : M // 2], hdh1[:].indirect(l2[:, 0 : M // 32]))
-        nc.scalar.activation(he1[:, M // 2 : M], hdh1[:].indirect(l2[:, M // 32 : M // 16]), ACT.Copy)
-        nc.scalar.activation(he3, hdh1[:].indirect(l4[:]), ACT.Copy)
-        centred_sq = sb.tile([P, J], F32, tag="hdh1")
-        nc.scalar.activation(centred_sq[:], sig_neg[:], ACT.Square, bias=1.0, scale=-2.0)
+        he1 = sb.tile([P, M], F32)
+        he2 = sb.tile([P, M], F32)
+        v1 = sb.tile([P, M], F32)
+        v2 = sb.tile([P, M], F32)
+        v3 = sb.tile([P, M], F32, tag="v3")
+        z = sb.tile([P, M], F32)
+        parts = [(slice(0, M // 2), slice(0, M // 32)), (slice(M // 2, M), slice(M // 32, M // 16))]
+        for cols, entries in parts:
+            nc.scalar.activation(he2[:, cols], hdh1[:].indirect(l3[:, entries]), ACT.Copy)
+            nc.scalar.activation(he1[:, cols], hdh1[:].indirect(l2[:, entries]), ACT.Copy)
+            nc.vector.tensor_tensor(v3[:, cols], hdh1[:].indirect(l4[:, entries]), e3[:, cols], mult)
+        inv_c = sb.tile([P, M], F32, tag="hdh1")
+        nc.scalar.activation(inv_c[:], c_sq, ACT.Abs_reciprocal_sqrt, bias=TINY)
+        for cols, entries in parts:
+            nc.vector.tensor_tensor(v2[:, cols], he2[:, cols], e2[:, cols], mult)
+            nc.vector.tensor_tensor(v1[:, cols], he1[:, cols], e1[:, cols], mult)
+            nc.vector.tensor_tensor(z[:, cols], v2[:, cols], v3[:, cols], add)
+            nc.vector.tensor_tensor(z[:, cols], z[:, cols], v1[:, cols], add)
+            nc.vector.tensor_tensor(z[:, cols], z[:, cols], rec[:, cols], mult)
+            for v, i, win, lst in ((v1, 1, win2, l2), (v2, 0, win3, l3)):
+                nc.vector.tensor_tensor(v[:, cols], z[:, cols], v[:, cols], sub)
+                nc.vector.tensor_tensor(v[:, cols], v[:, cols], inv[:, i, cols], mult)
+                nc.scalar.activation(win[:].indirect(lst[:, entries]), v[:, cols], ACT.Copy)
+        nc.vector.tensor_tensor(v3[:], z[:], v3[:], sub)
+        nc.vector.tensor_tensor(win4[:].indirect(l4[:]), v3[:], inv_c[:], mult)
 
-        x4 = sb.tile([P, 3, M], F32)
-        x2 = sb.tile([P, 3, M], F32)
-        x3 = sb.tile([P, 3, M], F32)
-
-        def finish(x, win, lst):
-            nc.vector.tensor_tensor(x[:, 0, :], x[:, 0, :], x[:, 1, :], add)
-            nc.vector.tensor_tensor(x[:, 0, :], x[:, 0, :], x[:, 2, :], sub)
-            nc.vector.tensor_tensor(x[:, 0, :], x[:, 0, :], gain[:], mult)
-            nc.scalar.activation(win[:].indirect(lst[:]), x[:, 0, :], ACT.Copy)
-
-        nc.vector.tensor_tensor(x4[:, 1, :], ha, he2, mult)
-        nc.vector.tensor_tensor(x4[:, 0, :], hb, he1, mult)
-        nc.vector.tensor_tensor(x4[:, 2, :], ab_sq[:], he3, mult)
-        finish(x4, win4, l4)
-        nc.vector.tensor_tensor(x2[:, 2, :], rest_sq[:, 0, :], he1, mult)
-        nc.vector.tensor_tensor(x2[:, 0, :], hc, he2, mult)
-        nc.vector.tensor_tensor(x2[:, 1, :], hb, he3, mult)
-        finish(x2, win2, l2)
-        nc.vector.tensor_tensor(x3[:, 2, :], rest_sq[:, 1, :], he2, mult)
-        nc.vector.tensor_tensor(x3[:, 0, :], hc, he1, mult)
-        nc.vector.tensor_tensor(x3[:, 1, :], ha, he3, mult)
-        finish(x3, win3, l3)
-
-        total = sb.tile([P, J], F32, tag="gain")
-        nc.vector.scalar_tensor_tensor(total[:], centred_sq[:], 1.0, dh1_sq[:], sub, mult)
+        for n in range(4):
+            cols = slice(n * J // 4, (n + 1) * J // 4)
+            nc.vector.scalar_tensor_tensor(total[:, cols], centred_sq[:, cols], 1.0, total[:, cols], sub, mult)
+        res = sb.tile([P, J], F32, tag="v3")
         for cols in halves:
-            nc.vector.tensor_tensor(total[:, cols], win4[:, cols], total[:, cols], sub)
-        for win in (win2, win3):
+            nc.vector.tensor_tensor(res[:, cols], win2[:, cols], total[:, cols], sub)
+        for win in (win4, win3):
             for cols in halves:
-                nc.vector.tensor_tensor(total[:, cols], total[:, cols], win[:, cols], add)
+                nc.vector.tensor_tensor(res[:, cols], res[:, cols], win[:, cols], add)
         for cols in halves:
-            nc.vector.scalar_tensor_tensor(total[:, cols], total[:, cols], og_t[:], sig[:, cols], mult, mult)
+            nc.vector.scalar_tensor_tensor(res[:, cols], res[:, cols], og_t[:], sig[:, cols], mult, mult)
         for cols in halves:
-            nc.vector.tensor_tensor(total[:, cols], total[:, cols], base_t[:, cols], add)
-            nc.sync.dma_start(out=out[:, cols], in_=total[:, cols])
+            nc.vector.tensor_tensor(res[:, cols], res[:, cols], base_t[:, cols], add)
+            nc.sync.dma_start(out=out[:, cols], in_=res[:, cols])

@@ -38,15 +38,15 @@ def tile_attend_gptriples_kernel(tc, tab_words, tab_scales, w1, bias, wo, dy, og
             engine_copy(out=dst.rearrange("p (c i) t -> p c t i", i=4), in_=src.rearrange("p t (c i) -> p c t i", i=4))
 
         scales = sb.tile([P, T], U8, align_bytes=64)
+        nc.vector.memset(scales[:].bitcast(I32), 0)
         l1 = lists.tile([P, J // 16], U16)
         nc.sync.dma_start(l1[:], offs)
-        for quad in range(4):
-            rows = tab_scales[0, 4 * quad : 4 * quad + 4, :].bitcast(I32)
-            nc.sync.dma_start(out=scales[32 * quad : 32 * quad + 32, :].bitcast(I32), in_=rows.partition_broadcast(8))
-        w1_raw = sb.tile([P, PACK, R], F32)
-        nc.sync.dma_start(out=w1_raw[:], in_=w1.rearrange("(p t) r -> p t r", t=PACK))
         words = sb.tile([P, T], U16, align_bytes=64)
         nc.sync.dma_start(out=words[:].bitcast(I32), in_=tab_words[0].bitcast(I32))
+        w1_raw = sb.tile([P, PACK, R], F32)
+        nc.sync.dma_start(out=w1_raw[:], in_=w1.rearrange("(p t) r -> p t r", t=PACK))
+        for quad in range(4):
+            nc.sync.dma_start(out=scales[32 * quad : 32 * quad + 4, :].bitcast(I32), in_=tab_scales[0, 4 * quad : 4 * quad + 4, :].bitcast(I32))
         bias_t = sb.tile([P, 1], F32)
         nc.sync.dma_start(out=bias_t[:], in_=bias)
         wo_raw = sb.tile([P, PACK, R], F32)
@@ -74,8 +74,8 @@ def tile_attend_gptriples_kernel(tc, tab_words, tab_scales, w1, bias, wo, dy, og
         nc.gpsimd.memset(warm_in[:], 1.0)
         warm_sig = sb.tile([P, 1], F32)
         nc.scalar.activation(warm_sig[:], warm_in[:], ACT.Sigmoid)
-        g_scales = sb.tile([P, J], U8, align_bytes=64)
-        nc.vector.tensor_copy(g_scales[:], scales[:].indirect(l1[:]))
+        g_words = sb.tile([P, J], U16, align_bytes=64)
+        nc.vector.tensor_copy(g_words[:], words[:].indirect(l1[:]))
         w1_bf = sb.tile([P, R, PACK], BF16, align_bytes=64)
         interleave(nc.scalar.copy, w1_bf[:], w1_raw[:])
         w1_codes = sb.tile([P, R], U32, align_bytes=64)
@@ -84,11 +84,11 @@ def tile_attend_gptriples_kernel(tc, tab_words, tab_scales, w1, bias, wo, dy, og
         neg_bias = sb.tile([P, 1], F32)
         nc.scalar.activation(neg_bias[:], bias_t[:], ACT.Copy, scale=-1.0)
 
-        g_words = sb.tile([P, J], U16, align_bytes=64)
+        g_scales = sb.tile([P, J], U8, align_bytes=64)
         sig_neg = sb.tile([P, J], F32)
         a_ps = []
         for n, cols in enumerate(halves):
-            nc.vector.tensor_copy(g_words[:, cols], words[:].indirect(l1[:, n * (HALF // 16) : (n + 1) * (HALF // 16)]))
+            nc.vector.tensor_copy(g_scales[:, cols], scales[:].indirect(l1[:, n * (HALF // 16) : (n + 1) * (HALF // 16)]))
             bank = ps.tile([P, HALF], F32, name="a_bank%d" % n)
             nc.tensor.matmul_mx(out=bank[:], lhsT=w1_codes[:].bitcast(FP8X4), lhsT_scale=w1_scales[:],
                                 rhs=g_words[:, cols].bitcast(FP4X4), rhs_scale=g_scales[:, cols], start=True, stop=True)

import math
from contextlib import ExitStack

import concourse.mybir as mybir

K, R, F, T, J, M = 512, 128, 512, 2048, 512, 256
FLOPS = 2 * K * R * J + 2 * F * R * M

F32 = mybir.dt.float32
BF16 = mybir.dt.bfloat16
I32 = mybir.dt.int32
U32 = mybir.dt.uint32
U16 = mybir.dt.uint16
U8 = mybir.dt.uint8
FP8X4 = mybir.dt.float8_e4m3fn_x4
FP4X4 = mybir.dt.float4_e2m1fn_x4
ALU = mybir.AluOpType
ACT = mybir.ActivationFunctionType

P = 128
PACK = 4
HALF = J // 2
SHARE = 64
TINY = 2.0 ** -63


def tile_attend_gptriples_kernel(tc, tab_words, tab_scales, w1, bias, wo, dy, og, base, offs, offs2, offs3, offs4, out):
    nc = tc.nc
    mult, add, sub, amax = ALU.mult, ALU.add, ALU.subtract, ALU.max
    halves = [slice(0, HALF), slice(HALF, J)]

    with ExitStack() as ctx:
        lists = ctx.enter_context(tc.tile_pool(name="lists", bufs=1))
        sb = ctx.enter_context(tc.tile_pool(name="sb", bufs=1))
        ps = ctx.enter_context(tc.psum_pool(name="ps", bufs=1))

        def interleave(engine_copy, dst, src):
            engine_copy(out=dst.rearrange("p (c i) t -> p c t i", i=4), in_=src.rearrange("p t (c i) -> p c t i", i=4))

        scales = sb.tile([P, T], U8, align_bytes=64)
        nc.vector.memset(scales[:].bitcast(I32), 0)
        l1 = lists.tile([P, J // 16], U16)
        nc.sync.dma_start(l1[:], offs)
        words = sb.tile([P, T], U16, align_bytes=64)
        nc.sync.dma_start(out=words[:].bitcast(I32), in_=tab_words[0].bitcast(I32))
        w1_raw = sb.tile([P, PACK, R], F32)
        nc.sync.dma_start(out=w1_raw[:], in_=w1.rearrange("(p t) r -> p t r", t=PACK))
        for quad in range(4):
            nc.sync.dma_start(out=scales[32 * quad : 32 * quad + 4, :].bitcast(I32), in_=tab_scales[0, 4 * quad : 4 * quad + 4, :].bitcast(I32))
        bias_t = sb.tile([P, 1], F32)
        nc.sync.dma_start(out=bias_t[:], in_=bias)
        wo_raw = sb.tile([P, PACK, R], F32)
        nc.sync.dma_start(out=wo_raw[:], in_=wo.rearrange("(p t) r -> p t r", t=PACK))
        dy_raw = sb.tile([P, PACK, M], F32, tag="dy_raw")
        nc.sync.dma_start(out=dy_raw[:], in_=dy.rearrange("(p t) m -> p t m", t=PACK))
        l2 = lists.tile([P, M // 16], U16)
        nc.sync.dma_start(l2[:], offs2)
        l3 = lists.tile([P, M // 16], U16)
        nc.sync.dma_start(l3[:], offs3)
        l4 = lists.tile([P, M // 16], U16)
        nc.sync.dma_start(l4[:], offs4)
        og_t = sb.tile([P, 1], F32)
        nc.sync.dma_start(out=og_t[:], in_=og)
        base_t = sb.tile([P, J], F32)
        nc.sync.dma_start(out=base_t[:], in_=base)

        win2 = sb.tile([P, J], F32)
        win3 = sb.tile([P, J], F32)
        win4 = sb.tile([P, J], F32)
        for win in (win2, win3, win4):
            nc.gpsimd.memset(win[:], 0.0)

        warm_in = sb.tile([P, 1], F32)
        nc.gpsimd.memset(warm_in[:], 1.0)
        warm_sig = sb.tile([P, 1], F32)
        nc.scalar.activation(warm_sig[:], warm_in[:], ACT.Sigmoid)
        g_words = sb.tile([P, J], U16, align_bytes=64)
        nc.vector.tensor_copy(g_words[:], words[:].indirect(l1[:]))
        w1_bf = sb.tile([P, R, PACK], BF16, align_bytes=64)
        interleave(nc.scalar.copy, w1_bf[:], w1_raw[:])
        w1_codes = sb.tile([P, R], U32, align_bytes=64)
        w1_scales = sb.tile([P, R], U8, align_bytes=64, tag="w1_scales")
        nc.vector.quantize_mx(out=w1_codes[:].bitcast(FP8X4), scales=w1_scales[:], in_=w1_bf[:].rearrange("p r t -> p (r t)"))
        neg_bias = sb.tile([P, 1], F32)
        nc.scalar.activation(neg_bias[:], bias_t[:], ACT.Copy, scale=-1.0)

        g_scales = sb.tile([P, J], U8, align_bytes=64)
        sig_neg = sb.tile([P, J], F32)
        a_ps = []
        for n, cols in enumerate(halves):
            nc.vector.tensor_copy(g_scales[:, cols], scales[:].indirect(l1[:, n * (HALF // 16) : (n + 1) * (HALF // 16)]))
            bank = ps.tile([P, HALF], F32, name="a_bank%d" % n)
            nc.tensor.matmul_mx(out=bank[:], lhsT=w1_codes[:].bitcast(FP8X4), lhsT_scale=w1_scales[:],
                                rhs=g_words[:, cols].bitcast(FP4X4), rhs_scale=g_scales[:, cols], start=True, stop=True)
            nc.scalar.activation(sig_neg[:, cols], bank[:], ACT.Sigmoid, bias=neg_bias[:], scale=-1.0)
            a_ps.append(bank)

        last_bf = sb.tile([P, R + M, PACK], BF16, align_bytes=64, tag="last_bf")
        interleave(nc.vector.tensor_copy, last_bf[:, 0:R, :], wo_raw[:])
        interleave(nc.vector.tensor_copy, last_bf[:, R : R + M, :], dy_raw[:])
        last_codes = sb.tile([P, R + M], U32, align_bytes=64)
        last_scales = sb.tile([P, R + M], U8, align_bytes=64)
        nc.vector.quantize_mx(out=last_codes[:].bitcast(FP8X4), scales=last_scales[:], in_=last_bf[:].rearrange("p c t -> p (c t)"))
        c0 = ps.tile([P, M], F32)
        nc.tensor.matmul_mx(out=c0[:], lhsT=last_codes[:, 0:R].bitcast(FP8X4), lhsT_scale=last_scales[:, 0:R],
                            rhs=last_codes[:, R : R + M].bitcast(FP8X4), rhs_scale=last_scales[:, R : R + M], start=True, stop=True)
        log_neg = [sb.tile([P, HALF], F32, align_bytes=64, tag="w1_scales", name="log0"), sb.tile([P, HALF], F32, tag="log1", name="log1")]
        pre = sb.tile([P, J], F32, tag="dy_raw")
        h1 = sb.tile([P, J], F32)
        for n, cols in enumerate(halves):
            nc.scalar.activation(log_neg[n][:], sig_neg[:, cols], ACT.Ln, bias=TINY)
            nc.vector.tensor_scalar(pre[:, cols], a_ps[n][:], bias_t[:], None, add)
        for n, cols in enumerate(halves):
            nc.vector.scalar_tensor_tensor(h1[:, cols], log_neg[n][:], -1.0, pre[:, cols], mult, amax)

        sig = sb.tile([P, J], F32, align_bytes=64, tag="last_bf")
        nc.vector.tensor_scalar(sig[:], sig_neg[:], -1.0, 1.0, mult, add)
        sig_sq = sb.tile([P, J], F32, tag="sig_sq")
        nc.vector.tensor_tensor(sig_sq[:], sig[:], sig[:], mult)

        hg = sb.tile([P, 3, M], F32)
        hc, hb, ha = hg[:, 0, :], hg[:, 1, :], hg[:, 2, :]
        nc.scalar.activation(ha, h1[:].indirect(l2[:]), ACT.Copy)
        warm_root = sb.tile([P, 1], F32, tag="log1")
        nc.scalar.activation(warm_root[:], warm_in[:], ACT.Abs_reciprocal_sqrt, bias=1.0)
        nc.vector.tensor_copy(hb, h1[:].indirect(l3[:]))
        nc.vector.tensor_copy(hc, h1[:].indirect(l4[:]))
        ab = sb.tile([P, M], F32)
        nc.vector.tensor_tensor(ab[:], ha, hb, mult)
        s = sb.tile([P, M], F32, tag="s")
        nc.vector.tensor_tensor(s[:], ab[:], hc, mult)
        root = sb.tile([P, M], F32)
        nc.scalar.activation(root[:], s[:], ACT.Abs_reciprocal_sqrt, bias=1.0)
        rec = sb.tile([P, M], F32)
        nc.scalar.activation(rec[:], root[:], ACT.Square)
        c_ab = sb.tile([P, M], F32)
        nc.vector.tensor_tensor(c_ab[:], c0[:], ab[:], mult)
        c_c = sb.tile([P, M], F32)
        nc.vector.tensor_tensor(c_c[:], c0[:], hc, mult)
        c_pair = sb.tile([P, 2, M], F32, tag="c_pair")
        c_bc, c_ac = c_pair[:, 0, :], c_pair[:, 1, :]
        nc.vector.tensor_tensor(c_pair[:], hg[:, 1:3, :], c_c[:].unsqueeze(1).to_broadcast([P, 2, M]), mult)

        e1 = sb.tile([P, M], F32)
        e2 = sb.tile([P, M], F32)
        e3 = sb.tile([P, M], F32)
        nc.vector.tensor_tensor(e3[:], c_ab[:], rec[:], mult)
        nc.scalar.activation(win4[:].indirect(l4[:]), e3[:], ACT.Copy)
        nc.vector.tensor_tensor(win3[:].indirect(l3[:, 0 : SHARE // 16]), c_ac[:, 0:SHARE], rec[:, 0:SHARE], mult)
        nc.vector.tensor_tensor(e2[:], c_ac, rec[:], mult)
        nc.scalar.activation(win3[:].indirect(l3[:, SHARE // 16 : M // 16]), e2[:, SHARE:M], ACT.Copy)
        nc.vector.tensor_tensor(win2[:].indirect(l2[:]), c_bc, rec[:], mult)
        dh1 = sb.tile([P, J], F32)
        for cols in halves:
            nc.vector.tensor_tensor(dh1[:, cols], win2[:, cols], win4[:, cols], add)
        nc.vector.tensor_tensor(e1[:], c_bc, rec[:], mult)
        early = sb.tile([P, M + J], F32, tag="s")
        c_sq, centred_sq = early[:, 0:M], early[:, M : M + J]
        nc.scalar.activation(c_sq, hc, ACT.Square)
        nc.scalar.activation(centred_sq, sig_neg[:], ACT.Square, bias=1.0, scale=-2.0)
        ba_sq = sb.tile([P, 2, M], F32, tag="c_pair")
        nc.scalar.activation(ba_sq[:], hg[:, 1:3, :], ACT.Square)
        inv = sb.tile([P, 2, M], F32)
        nc.scalar.activation(inv[:], ba_sq[:], ACT.Abs_reciprocal_sqrt, bias=TINY)
        for cols in halves:
            nc.vector.tensor_tensor(dh1[:, cols], dh1[:, cols], win3[:, cols], add)
        hdh1 = sb.tile([P, J], F32, tag="hdh1")
        for cols in halves:
            nc.vector.scalar_tensor_tensor(hdh1[:, cols], dh1[:, cols], 2.0, sig_sq[:, cols], mult, mult)
        total = sb.tile([P, J], F32)
        nc.scalar.activation(total[:], dh1[:], ACT.Square, scale=math.sqrt(0.5))

        he1 = sb.tile([P, M], F32)
        he2 = sb.tile([P, M], F32)
        v1 = sb.tile([P, M], F32)
        v2 = sb.tile([P, M], F32)
        v3 = sb.tile([P, M], F32, tag="v3")
        z = sb.tile([P, M], F32)
        parts = [(slice(0, M // 2), slice(0, M // 32)), (slice(M // 2, M), slice(M // 32, M // 16))]
        for cols, entries in parts:
            nc.scalar.activation(he2[:, cols], hdh1[:].indirect(l3[:, entries]), ACT.Copy)
            nc.scalar.activation(he1[:, cols], hdh1[:].indirect(l2[:, entries]), ACT.Copy)
            nc.vector.tensor_tensor(v3[:, cols], hdh1[:].indirect(l4[:, entries]), e3[:, cols], mult)
        inv_c = sb.tile([P, M], F32, tag="hdh1")
        nc.scalar.activation(inv_c[:], c_sq, ACT.Abs_reciprocal_sqrt, bias=TINY)
        for cols, entries in parts:
            nc.vector.tensor_tensor(v2[:, cols], he2[:, cols], e2[:, cols], mult)
            nc.vector.tensor_tensor(v1[:, cols], he1[:, cols], e1[:, cols], mult)
            nc.vector.tensor_tensor(z[:, cols], v2[:, cols], v3[:, cols], add)
            nc.vector.tensor_tensor(z[:, cols], z[:, cols], v1[:, cols], add)
            nc.vector.tensor_tensor(z[:, cols], z[:, cols], rec[:, cols], mult)
            for v, i, win, lst in ((v1, 1, win2, l2), (v2, 0, win3, l3)):
                nc.vector.tensor_tensor(v[:, cols], z[:, cols], v[:, cols], sub)
                nc.vector.tensor_tensor(v[:, cols], v[:, cols], inv[:, i, cols], mult)
                nc.scalar.activation(win[:].indirect(lst[:, entries]), v[:, cols], ACT.Copy)
        nc.vector.tensor_tensor(v3[:], z[:], v3[:], sub)
        nc.vector.tensor_tensor(win4[:].indirect(l4[:]), v3[:], inv_c[:], mult)

        for n in range(4):
            cols = slice(n * J // 4, (n + 1) * J // 4)
            nc.vector.scalar_tensor_tensor(total[:, cols], centred_sq[:, cols], 1.0, total[:, cols], sub, mult)
        res = sb.tile([P, J], F32, tag="v3")
        for cols in halves:
            nc.vector.tensor_tensor(res[:, cols], win2[:, cols], total[:, cols], sub)
        for win in (win4, win3):
            for cols in halves:
                nc.vector.tensor_tensor(res[:, cols], res[:, cols], win[:, cols], add)
        for cols in halves:
            nc.vector.scalar_tensor_tensor(res[:, cols], res[:, cols], og_t[:], sig[:, cols], mult, mult)
        for cols in halves:
            nc.vector.tensor_tensor(res[:, cols], res[:, cols], base_t[:, cols], add)
            nc.sync.dma_start(out=out[:, cols], in_=res[:, cols])
